import numpy as np
import ml_dtypes


def mxq(x, axis, fmt="e4m3"):
    dtype, down = {"e4m3": (ml_dtypes.float8_e4m3fn, 7), "e5m2": (ml_dtypes.float8_e5m2, 14)}[fmt]
    v = np.moveaxis(np.asarray(x, np.float32).astype(ml_dtypes.bfloat16).astype(np.float64), axis, -1)
    blocks = v.reshape(v.shape[:-1] + (-1, 32))
    amax = np.abs(blocks).max(-1, keepdims=True)
    byte = np.maximum(np.where(amax > 0, np.frexp(amax)[1] - 1 + 127, 0) - down, 1)
    scale = np.exp2(byte - 127.0)
    codes = (blocks / scale).astype(np.float32).astype(dtype).astype(np.float64)
    return np.moveaxis((codes * scale).reshape(v.shape), -1, axis)


WIDE = False


def mx_kscale(k):
    if not WIDE:
        return np.ones(k)
    levels = np.array([10, -10, 5, -5, 0])
    if k % 512:
        return np.exp2(np.random.permutation(np.resize(levels, k // 32))).repeat(32)
    a = np.empty((k // 512, 16))
    for p in range(k // 512):
        a[p, :8] = np.random.permutation(np.resize(levels, 8))
        for g in range(8):
            far = levels[np.abs(levels - a[p, g]) >= 10]
            a[p, g + 8] = far[np.random.randint(len(far))]
    return np.exp2(a.ravel()).repeat(32)


def f64(x):
    return np.asarray(x).astype(np.float64)


def striped(idx):
    return np.tile(idx.reshape(-1, 16).T, (8, 1)).astype(np.uint16)


def unstriped(offs):
    return offs[:16].T.reshape(-1).astype(np.int64)


def pack_weight(w):
    k, n = w.shape
    w = f64(np.asarray(w, np.float32).astype(ml_dtypes.bfloat16)).reshape(k // 32, 32, n)
    amax = np.abs(w).max(1)
    byte = np.clip(np.where(amax > 0, np.frexp(amax)[1] - 1 + 127 - 7, 1), 1, 254)
    scaled = (w * np.exp2(127.0 - byte)[:, None, :]).reshape(k, n).astype(np.float32)
    words = np.ascontiguousarray(scaled.reshape(k // 512, 128, 4, n).transpose(0, 1, 3, 2)).astype(ml_dtypes.float8_e4m3fn).view(np.uint8)
    return words, np.ascontiguousarray(byte.astype(np.uint8).reshape(k // 512, 16, n))


def unpack_weight(words, scales):
    g, p, n, _ = words.shape
    vals = np.ascontiguousarray(words).view(ml_dtypes.float8_e4m3fn).astype(np.float64) * np.repeat(np.exp2(scales.astype(np.float64) - 127.0), 8, axis=1)[..., None]
    return vals.transpose(0, 1, 3, 2).reshape(g * 512, n)


def silu(v):
    return v / (1.0 + np.exp(-np.maximum(v, -700.0)))


K, T, S, D, N, H = 512, 1024, 512, 4, 128, 512
P = 2 ** 7


def setup_inputs():
    n = np.random.standard_normal
    s = mx_kscale(K)[:, None]
    u = mx_kscale(H)
    packed_xT = pack_weight(n((K, T)) * s)
    return {
        "x_words": packed_xT[0],
        "x_scales": packed_xT[1],
        "w1": (n((K, H)) / np.sqrt(K) / s).astype(np.float32),
        "wg": (n((K, H)) / np.sqrt(K) / s).astype(np.float32),
        "stat": (np.tile(np.random.uniform(0.1, 0.5, S), (P, 1))).astype(np.float32),
        "depth": (np.tile(np.random.uniform(0.3, 1.2, S), (P, 1))).astype(np.float32),
        "unit": (np.random.uniform(0.5, 1.5, (H, 1)) * u[:, None]).astype(np.float32),
        "wo": (n((H, N)) / np.sqrt(H) / u[:, None]).astype(np.float32),
        "offs": striped(np.random.permutation(T)[:S]),
    }


def reference(x_words, x_scales, w1, wg, stat, depth, unit, wo, offs):
    xq = unpack_weight(x_words, x_scales)[:, unstriped(offs)]
    gt = np.tanh(mxq(f64(wg), 0, "e4m3").T @ xq)
    al = gt * (0.5 * f64(stat)[:1]) + f64(stat)[:1]
    hs = mxq(f64(w1), 0, "e4m3").T @ xq
    ah = al * hs
    inp = ah.reshape(len(ah), -1, D).sum(axis=2)
    mid = silu(inp)
    strm = np.repeat(mid, D, axis=1) * f64(depth)[:1] + hs * (gt + 1.0)
    zz = f64(unit) * strm
    return mxq(f64(wo), 0, "e4m3").T @ mxq(zz, 0, "e4m3")

@@ -1,0 +1,194 @@
+from contextlib import ExitStack
+
+import concourse.mybir as mybir
+from concourse.masks import make_identity
+
+F32 = mybir.dt.float32
+BF16 = mybir.dt.bfloat16
+I32 = mybir.dt.int32
+U32 = mybir.dt.uint32
+U16 = mybir.dt.uint16
+U8 = mybir.dt.uint8
+FP8X4 = mybir.dt.float8_e4m3fn_x4
+ACT = mybir.ActivationFunctionType
+ALU = mybir.AluOpType
+
+P = 128
+PACK = 4
+K, T, S, D, N, H = 512, 1024, 512, 4, 128, 512
+V = S // D
+HALF = H // 2
+FLOPS = 2 * K * H * S * 2 + 2 * H * N * S
+
+
+def tile_picked_yhyper_back_p_kernel(
+    tc, x_words, x_scales, w1, wg, stat, depth, unit, wo, offs, out
+):
+    nc = tc.nc
+    with ExitStack() as ctx:
+        sb = ctx.enter_context(tc.tile_pool(name="sb", bufs=1))
+        ps = ctx.enter_context(tc.psum_pool(name="ps", bufs=1))
+
+        def tile(name, shape, dtype):
+            return sb.tile(shape, dtype, name=name, align_bytes=64)
+
+        def bank(name, tag):
+            return ps.tile([P, 512], F32, name=name, tag=tag)
+
+        offsets = sb.tile([P, S // 16], U16, name="offsets")
+        xw = tile("xw", [P, T], U32)
+        xs = tile("xs", [P, T], U8)
+        nc.vector.memset(xs[:].bitcast(I32), 0)
+        nc.sync.dma_start(out=xw[:].bitcast(I32), in_=x_words[0].rearrange("p n t -> p (n t)").bitcast(I32))
+        nc.sync.dma_start(offsets[:], offs)
+        for q in range(4):
+            nc.scalar.dma_start(
+                out=xs[32 * q : 32 * q + 4, :].bitcast(I32), in_=x_scales[0, 4 * q : 4 * q + 4, :].bitcast(I32)
+            )
+        raws = {}
+        for name, w in (("wg", wg), ("w1", w1)):
+            for h in range(2):
+                raw = tile(f"{name}_raw{h}", [P, PACK, HALF], F32)
+                nc.sync.dma_start(out=raw[:], in_=w[:, h * HALF : (h + 1) * HALF].rearrange("(p j) c -> p j c", j=PACK))
+                raws[name, h] = raw
+        stat4 = tile("stat4", [P, D], F32)
+        nc.sync.dma_start(out=stat4[:], in_=stat[0, :].rearrange("(v d) -> v d", d=D))
+        wo_raw = tile("wo_raw", [P, PACK, N], F32)
+        nc.sync.dma_start(out=wo_raw[:], in_=wo.rearrange("(p j) c -> p j c", j=PACK))
+        depth4 = tile("depth4", [P, D], F32)
+        nc.sync.dma_start(out=depth4[:], in_=depth[0, :].rearrange("(v d) -> v d", d=D))
+        unit4 = tile("unit4", [P, PACK], F32)
+        nc.sync.dma_start(out=unit4[:], in_=unit.rearrange("(p t) o -> p (t o)", t=PACK))
+
+        ident = tile("ident", [P, P], F32)
+        make_identity(nc, ident[:])
+        warm = tile("warm", [P, 1], F32)
+        nc.scalar.activation(warm[:], ident[:, 0:1], ACT.Silu)
+
+        xg = tile("xg", [P, S], U32)
+        nc.vector.tensor_copy(xg[:].rearrange("p (d v) -> p v d", d=D), xw[:].indirect(offsets[:]))
+        sg = tile("sg", [P, S], U8)
+        nc.vector.tensor_copy(sg[:], xs[:].indirect(offsets[:]))
+        sd = tile("sd", [P, S], U8)
+        nc.vector.tensor_copy(sd[:].rearrange("p (d v) -> p d v", d=D), sg[:].rearrange("p (v d) -> p d v", d=D))
+
+        def cast(engine, name, raw, width):
+            grouped = tile(name, [P, width, PACK], BF16)
+            dst = grouped[:].rearrange("p (c i) t -> p c t i", i=4)
+            src = raw[:].rearrange("p t (c i) -> p c t i", i=4)
+            if engine == "scalar":
+                nc.scalar.copy(dst, src)
+            else:
+                nc.vector.tensor_copy(dst, src)
+            return grouped
+
+        def quantize(codes, scales, grouped):
+            nc.vector.quantize_mx(out=codes.bitcast(FP8X4), scales=scales, in_=grouped[:].rearrange("p c t -> p (c t)"))
+
+        wq = {}
+        for name in ("wg", "w1"):
+            codes = tile(f"{name}_codes", [P, H], U32)
+            scales = tile(f"{name}_scales", [P, H], U8)
+            for h in range(2):
+                engine = "vector" if (name, h) == ("w1", 1) else "scalar"
+                grouped = cast(engine, f"{name}_bf{h}", raws[name, h], HALF)
+                cols = slice(h * HALF, (h + 1) * HALF)
+                quantize(codes[:, cols], scales[:, cols], grouped)
+            wq[name] = (codes, scales)
+
+        def product(acc, name, d):
+            cols = slice(d * V, (d + 1) * V)
+            nc.tensor.matmul_mx(
+                out=acc[:],
+                lhsT=xg[:, cols].bitcast(FP8X4),
+                lhsT_scale=sd[:, cols],
+                rhs=wq[name][0][:].bitcast(FP8X4),
+                rhs_scale=wq[name][1][:],
+                start=True,
+                stop=True,
+            )
+
+        def dealt(acc):
+            return acc[:].rearrange("p (m t) -> p t m", t=PACK)
+
+        def planes(t3):
+            return t3[:].rearrange("p (t m) -> p t m", t=PACK)
+
+        gates = []
+        for d in range(D):
+            acc = bank(f"g{d}", f"a{d}")
+            product(acc, "wg", d)
+            gate = tile(f"gate{d}", [P, H], F32)
+            nc.scalar.activation(planes(gate), dealt(acc), ACT.Tanh)
+            gates.append(gate)
+
+        zbanks = []
+
+        def turn(d, src, first, last):
+            for t in range(PACK):
+                nc.tensor.matmul(
+                    zbanks[d][:, t * P : (t + 1) * P],
+                    src[:, t * P : (t + 1) * P],
+                    ident[:],
+                    start=(first and t == 0),
+                    stop=(last and t == PACK - 1),
+                    is_transpose=True,
+                )
+
+        mix = None
+        for d in range(D):
+            acc = bank(f"h{d}", f"b{d}")
+            product(acc, "w1", d)
+            both = tile(f"both{d}", [P, H], F32)
+            nc.vector.scalar_tensor_tensor(planes(both), planes(gates[d]), 2.0, dealt(acc), ALU.add, ALU.mult)
+            neg = tile(f"neg{d}", [P, H], F32)
+            nc.scalar.activation(planes(neg), dealt(acc), ACT.Copy, scale=-1.0)
+            nxt = tile(f"mix{d}", [P, H], F32)
+            if d == 0:
+                nc.vector.tensor_scalar(nxt[:], both[:], stat4[:, 0:1], None, ALU.mult)
+            else:
+                nc.vector.scalar_tensor_tensor(nxt[:], both[:], stat4[:, d : d + 1], mix[:], ALU.mult, ALU.add)
+            mix = nxt
+            zbanks.append(bank(f"z{d}", f"a{d}"))
+            turn(d, both, True, False)
+            turn(d, neg, False, False)
+
+        wo_bf = cast("scalar", "wo_bf", wo_raw, N)
+        wo_codes = tile("wo_codes", [P, N], U32)
+        wo_scales = tile("wo_scales", [P, N], U8)
+        quantize(wo_codes[:], wo_scales[:], wo_bf)
+
+        mid = tile("mid", [P, H], F32)
+        nc.scalar.activation(mid[:], mix[:], ACT.Silu, scale=0.5)
+
+        obank = bank("o", "b0")
+        for d in range(D):
+            back = tile(f"back{d}", [P, H], F32)
+            if d == 0:
+                nc.vector.tensor_scalar(back[:], mid[:], depth4[:, 0:1], None, ALU.mult)
+            else:
+                nc.scalar.activation(back[:], mid[:], ACT.Copy, scale=depth4[:, d : d + 1])
+            turn(d, back, False, True)
+        for d in range(D):
+            zz = tile(f"zz{d}", [P, V, PACK], BF16)
+            nc.vector.tensor_tensor(
+                zz[:],
+                zbanks[d][:].rearrange("p (t v) -> p v t", t=PACK),
+                unit4[:].unsqueeze(1).to_broadcast([P, V, PACK]),
+                ALU.mult,
+            )
+            z_codes = tile(f"z_codes{d}", [P, V], U32)
+            z_scales = tile(f"z_scales{d}", [P, V], U8)
+            quantize(z_codes[:], z_scales[:], zz)
+            nc.tensor.matmul_mx(
+                out=obank[:, d * V : (d + 1) * V],
+                lhsT=wo_codes[:].bitcast(FP8X4),
+                lhsT_scale=wo_scales[:],
+                rhs=z_codes[:].bitcast(FP8X4),
+                rhs_scale=z_scales[:],
+                start=True,
+                stop=True,
+            )
+        result = tile("result", [P, V, D], F32)
+        nc.scalar.copy(result[:], obank[:].rearrange("p (d v) -> p v d", d=D))
+        nc.sync.dma_start(out=out, in_=result[:].rearrange("p v d -> p (v d)"))

@@ -38,11 +38,13 @@ def tile_picked_yhyper_back_p_kernel(
         offsets = sb.tile([P, S // 16], U16, name="offsets")
         xw = tile("xw", [P, T], U32)
         xs = tile("xs", [P, T], U8)
-        nc.vector.memset(xs[:].bitcast(I32), 0)
+        nc.gpsimd.memset(xs[:].bitcast(I32), 0)
+        zero = tile("zero", [P, 1], F32)
+        nc.gpsimd.memset(zero[:], 0.0)
         nc.sync.dma_start(out=xw[:].bitcast(I32), in_=x_words[0].rearrange("p n t -> p (n t)").bitcast(I32))
         nc.sync.dma_start(offsets[:], offs)
         for q in range(4):
-            nc.scalar.dma_start(
+            nc.sync.dma_start(
                 out=xs[32 * q : 32 * q + 4, :].bitcast(I32), in_=x_scales[0, 4 * q : 4 * q + 4, :].bitcast(I32)
             )
         raws = {}
@@ -63,7 +65,7 @@ def tile_picked_yhyper_back_p_kernel(
         ident = tile("ident", [P, P], F32)
         make_identity(nc, ident[:])
         warm = tile("warm", [P, 1], F32)
-        nc.scalar.activation(warm[:], ident[:, 0:1], ACT.Silu)
+        nc.scalar.activation(warm[:], zero[:], ACT.Silu)
 
         xg = tile("xg", [P, S], U32)
         nc.vector.tensor_copy(xg[:].rearrange("p (d v) -> p v d", d=D), xw[:].indirect(offsets[:]))
@@ -72,38 +74,42 @@ def tile_picked_yhyper_back_p_kernel(
         sd = tile("sd", [P, S], U8)
         nc.vector.tensor_copy(sd[:].rearrange("p (d v) -> p d v", d=D), sg[:].rearrange("p (v d) -> p d v", d=D))
 
-        def cast(engine, name, raw, width):
+        def cast(name, raw, width, on_vector):
             grouped = tile(name, [P, width, PACK], BF16)
             dst = grouped[:].rearrange("p (c i) t -> p c t i", i=4)
             src = raw[:].rearrange("p t (c i) -> p c t i", i=4)
-            if engine == "scalar":
-                nc.scalar.copy(dst, src)
-            else:
-                nc.vector.tensor_copy(dst, src)
+            cut = on_vector // 4
+            if cut > 0:
+                nc.vector.tensor_copy(dst[:, :cut], src[:, :cut])
+            if on_vector < width:
+                nc.scalar.copy(dst[:, cut:], src[:, cut:])
             return grouped
 
         def quantize(codes, scales, grouped):
             nc.vector.quantize_mx(out=codes.bitcast(FP8X4), scales=scales, in_=grouped[:].rearrange("p c t -> p (c t)"))
 
+        on_vector = {("wg", 0): 0, ("wg", 1): 0, ("w1", 0): 128, ("w1", 1): 160}
         wq = {}
         for name in ("wg", "w1"):
             codes = tile(f"{name}_codes", [P, H], U32)
             scales = tile(f"{name}_scales", [P, H], U8)
             for h in range(2):
-                engine = "vector" if (name, h) == ("w1", 1) else "scalar"
-                grouped = cast(engine, f"{name}_bf{h}", raws[name, h], HALF)
+                grouped = cast(f"{name}_bf{h}", raws[name, h], HALF, on_vector[name, h])
                 cols = slice(h * HALF, (h + 1) * HALF)
                 quantize(codes[:, cols], scales[:, cols], grouped)
             wq[name] = (codes, scales)
 
-        def product(acc, name, d):
+        halves = [slice(0, HALF), slice(HALF, H)]
+        whole = slice(0, H)
+
+        def product(acc, name, d, part):
             cols = slice(d * V, (d + 1) * V)
             nc.tensor.matmul_mx(
-                out=acc[:],
+                out=acc[:, part],
                 lhsT=xg[:, cols].bitcast(FP8X4),
                 lhsT_scale=sd[:, cols],
-                rhs=wq[name][0][:].bitcast(FP8X4),
-                rhs_scale=wq[name][1][:],
+                rhs=wq[name][0][:, part].bitcast(FP8X4),
+                rhs_scale=wq[name][1][:, part],
                 start=True,
                 stop=True,
             )
@@ -114,13 +120,18 @@ def tile_picked_yhyper_back_p_kernel(
         def planes(t3):
             return t3[:].rearrange("p (t m) -> p t m", t=PACK)
 
-        gates = []
+        gbanks = [bank(f"g{d}", f"a{d}") for d in range(D)]
+        hbanks = [bank(f"h{d}", f"b{d}") for d in range(D)]
+        gates = [tile(f"gate{d}", [P, H], F32) for d in range(D)]
+        for banks, name in ((gbanks, "wg"), (hbanks, "w1")):
+            for part in halves:
+                for d in (0, 1):
+                    product(banks[d], name, d, part)
+        for d in (2, 3):
+            product(gbanks[d], "wg", d, whole)
+            product(hbanks[d], "w1", d, whole)
         for d in range(D):
-            acc = bank(f"g{d}", f"a{d}")
-            product(acc, "wg", d)
-            gate = tile(f"gate{d}", [P, H], F32)
-            nc.scalar.activation(planes(gate), dealt(acc), ACT.Tanh)
-            gates.append(gate)
+            nc.scalar.activation(planes(gates[d]), dealt(gbanks[d]), ACT.Tanh)
 
         zbanks = []
 
@@ -135,60 +146,102 @@ def tile_picked_yhyper_back_p_kernel(
                     is_transpose=True,
                 )
 
-        mix = None
-        for d in range(D):
-            acc = bank(f"h{d}", f"b{d}")
-            product(acc, "w1", d)
+        boths = []
+        mixes = [tile(f"mix{d}", [P, H], F32) for d in range(D)]
+
+        def stream(d):
+            acc = hbanks[d]
             both = tile(f"both{d}", [P, H], F32)
             nc.vector.scalar_tensor_tensor(planes(both), planes(gates[d]), 2.0, dealt(acc), ALU.add, ALU.mult)
             neg = tile(f"neg{d}", [P, H], F32)
             nc.scalar.activation(planes(neg), dealt(acc), ACT.Copy, scale=-1.0)
-            nxt = tile(f"mix{d}", [P, H], F32)
-            if d == 0:
-                nc.vector.tensor_scalar(nxt[:], both[:], stat4[:, 0:1], None, ALU.mult)
-            else:
-                nc.vector.scalar_tensor_tensor(nxt[:], both[:], stat4[:, d : d + 1], mix[:], ALU.mult, ALU.add)
-            mix = nxt
+            boths.append(both)
             zbanks.append(bank(f"z{d}", f"a{d}"))
             turn(d, both, True, False)
             turn(d, neg, False, False)
 
-        wo_bf = cast("scalar", "wo_bf", wo_raw, N)
+        def mix_in(d, cols):
+            nc.vector.scalar_tensor_tensor(
+                mixes[d][:, cols], boths[d][:, cols], stat4[:, d : d + 1], mixes[d - 1][:, cols], ALU.mult, ALU.add
+            )
+
+        stream(0)
+        nc.gpsimd.tensor_scalar(mixes[0][:], boths[0][:], stat4[:, 0:1], 0.0, ALU.mult, ALU.add)
+        stream(1)
+        stream(2)
+        mix_in(1, slice(0, H))
+        stream(3)
+        for d in (2, 3):
+            for cols in halves:
+                mix_in(d, cols)
+
+        wo_bf = cast("wo_bf", wo_raw, N, 0)
         wo_codes = tile("wo_codes", [P, N], U32)
         wo_scales = tile("wo_scales", [P, N], U8)
         quantize(wo_codes[:], wo_scales[:], wo_bf)
 
         mid = tile("mid", [P, H], F32)
-        nc.scalar.activation(mid[:], mix[:], ACT.Silu, scale=0.5)
+        for cols in halves:
+            nc.scalar.activation(mid[:, cols], mixes[3][:, cols], ACT.Silu, scale=0.5)
 
-        obank = bank("o", "b0")
+        obanks = [bank("o0", "b0"), bank("o1", "b1")]
         for d in range(D):
             back = tile(f"back{d}", [P, H], F32)
             if d == 0:
-                nc.vector.tensor_scalar(back[:], mid[:], depth4[:, 0:1], None, ALU.mult)
+                for cols in halves:
+                    nc.vector.tensor_scalar(back[:, cols], mid[:, cols], depth4[:, 0:1], None, ALU.mult)
+            elif d == 1:
+                nc.vector.tensor_scalar(back[:], mid[:], depth4[:, 1:2], None, ALU.mult)
             else:
                 nc.scalar.activation(back[:], mid[:], ACT.Copy, scale=depth4[:, d : d + 1])
             turn(d, back, False, True)
-        for d in range(D):
-            zz = tile(f"zz{d}", [P, V, PACK], BF16)
+        VH = V // 2
+        zzs = [tile(f"zz{d}", [P, V, PACK], BF16) for d in range(D)]
+        z_codes = [tile(f"z_codes{d}", [P, V], U32) for d in range(D)]
+        z_scales = [tile(f"z_scales{d}", [P, V], U8) for d in range(D)]
+
+        def scale_out(d, vs):
+            n = vs.stop - vs.start
             nc.vector.tensor_tensor(
-                zz[:],
-                zbanks[d][:].rearrange("p (t v) -> p v t", t=PACK),
-                unit4[:].unsqueeze(1).to_broadcast([P, V, PACK]),
+                zzs[d][:, vs, :],
+                zbanks[d][:].rearrange("p (t v) -> p v t", t=PACK)[:, vs, :],
+                unit4[:].unsqueeze(1).to_broadcast([P, n, PACK]),
                 ALU.mult,
             )
-            z_codes = tile(f"z_codes{d}", [P, V], U32)
-            z_scales = tile(f"z_scales{d}", [P, V], U8)
-            quantize(z_codes[:], z_scales[:], zz)
-            nc.tensor.matmul_mx(
-                out=obank[:, d * V : (d + 1) * V],
-                lhsT=wo_codes[:].bitcast(FP8X4),
-                lhsT_scale=wo_scales[:],
-                rhs=z_codes[:].bitcast(FP8X4),
-                rhs_scale=z_scales[:],
-                start=True,
-                stop=True,
+
+        def readout(d, vs):
+            nc.vector.quantize_mx(
+                out=z_codes[d][:, vs].bitcast(FP8X4),
+                scales=z_scales[d][:, vs],
+                in_=zzs[d][:, vs, :].rearrange("p c t -> p (c t)"),
             )
-        result = tile("result", [P, V, D], F32)
-        nc.scalar.copy(result[:], obank[:].rearrange("p (d v) -> p v d", d=D))
-        nc.sync.dma_start(out=out, in_=result[:].rearrange("p v d -> p (v d)"))
+            for g in range(vs.start // VH, vs.stop // VH):
+                nc.tensor.matmul_mx(
+                    out=obanks[g][:, d * VH : (d + 1) * VH],
+                    lhsT=wo_codes[:].bitcast(FP8X4),
+                    lhsT_scale=wo_scales[:],
+                    rhs=z_codes[d][:, g * VH : (g + 1) * VH].bitcast(FP8X4),
+                    rhs_scale=z_scales[d][:, g * VH : (g + 1) * VH],
+                    start=True,
+                    stop=True,
+                )
+
+        scale_out(0, slice(0, V))
+        for d in range(1, D - 1):
+            scale_out(d, slice(0, V))
+            readout(d - 1, slice(0, V))
+        scale_out(D - 1, slice(0, VH))
+        readout(D - 2, slice(0, V))
+        scale_out(D - 1, slice(VH, V))
+        readout(D - 1, slice(0, VH))
+        readout(D - 1, slice(VH, V))
+        for g in range(2):
+            result = tile(f"result{g}", [P, VH, D], F32)
+            src = obanks[g][:, : D * VH].rearrange("p (d v) -> p v d", d=D)
+            if g == 0:
+                nc.scalar.copy(result[:], src)
+                queue = nc.scalar
+            else:
+                nc.vector.tensor_copy(result[:], src)
+                queue = nc.sync
+            queue.dma_start(out=out[:, g * HALF : (g + 1) * HALF], in_=result[:].rearrange("p v d -> p (v d)"))

@@ -29,8 +29,8 @@ def tile_picked_yhyper_back_p_kernel(
         sb = ctx.enter_context(tc.tile_pool(name="sb", bufs=1))
         ps = ctx.enter_context(tc.psum_pool(name="ps", bufs=1))
 
-        def tile(name, shape, dtype):
-            return sb.tile(shape, dtype, name=name, align_bytes=64)
+        def tile(name, shape, dtype, tag=None):
+            return sb.tile(shape, dtype, name=name, tag=tag or name, align_bytes=64)
 
         def bank(name, tag):
             return ps.tile([P, 512], F32, name=name, tag=tag)
@@ -102,10 +102,10 @@ def tile_picked_yhyper_back_p_kernel(
         halves = [slice(0, HALF), slice(HALF, H)]
         whole = slice(0, H)
 
-        def product(acc, name, d, part):
+        def product(dst, name, d, part):
             cols = slice(d * V, (d + 1) * V)
             nc.tensor.matmul_mx(
-                out=acc[:, part],
+                out=dst,
                 lhsT=xg[:, cols].bitcast(FP8X4),
                 lhsT_scale=sd[:, cols],
                 rhs=wq[name][0][:, part].bitcast(FP8X4),
@@ -115,25 +115,29 @@ def tile_picked_yhyper_back_p_kernel(
             )
 
         def dealt(acc):
-            return acc[:].rearrange("p (m t) -> p t m", t=PACK)
+            return acc.rearrange("p (m t) -> p t m", t=PACK)
 
         def planes(t3):
             return t3[:].rearrange("p (t m) -> p t m", t=PACK)
 
-        gbanks = [bank(f"g{d}", f"a{d}") for d in range(D)]
+        gbanks = [bank(f"g{d}", f"a{d}") for d in range(2)]
         hbanks = [bank(f"h{d}", f"b{d}") for d in range(D)]
         gates = [tile(f"gate{d}", [P, H], F32) for d in range(D)]
-        for banks, name in ((gbanks, "wg"), (hbanks, "w1")):
-            for part in halves:
-                for d in (0, 1):
-                    product(banks[d], name, d, part)
+        for part in halves:
+            for d in (0, 1):
+                product(gbanks[d][:, part], "wg", d, part)
+        for h in range(2):
+            for d in (0, 1):
+                product(hbanks[h][:, halves[d]], "w1", d, halves[h])
+        for d in (0, 1):
+            nc.scalar.activation(planes(gates[d]), dealt(gbanks[d][:]), ACT.Tanh)
         for d in (2, 3):
-            product(gbanks[d], "wg", d, whole)
-            product(hbanks[d], "w1", d, whole)
-        for d in range(D):
-            nc.scalar.activation(planes(gates[d]), dealt(gbanks[d]), ACT.Tanh)
+            gbanks.append(bank(f"g{d}", f"a{d - 2}"))
+            product(gbanks[d][:], "wg", d, whole)
+            product(hbanks[d][:], "w1", d, whole)
+            nc.scalar.activation(planes(gates[d]), dealt(gbanks[d][:]), ACT.Tanh)
 
-        zbanks = []
+        zbanks = [bank(f"z{d}", f"a{(d + 2) % D}") for d in range(D)]
 
         def turn(d, src, first, last):
             for t in range(PACK):
@@ -146,37 +150,54 @@ def tile_picked_yhyper_back_p_kernel(
                     is_transpose=True,
                 )
 
-        boths = []
+        boths = [tile(f"both{d}", [P, H], F32) for d in range(D)]
+        negs = [tile(f"neg{d}", [P, H], F32) for d in range(D)]
         mixes = [tile(f"mix{d}", [P, H], F32) for d in range(D)]
+        MH = P // 2
 
-        def stream(d):
-            acc = hbanks[d]
-            both = tile(f"both{d}", [P, H], F32)
-            nc.vector.scalar_tensor_tensor(planes(both), planes(gates[d]), 2.0, dealt(acc), ALU.add, ALU.mult)
-            neg = tile(f"neg{d}", [P, H], F32)
-            nc.scalar.activation(planes(neg), dealt(acc), ACT.Copy, scale=-1.0)
-            boths.append(both)
-            zbanks.append(bank(f"z{d}", f"a{d}"))
-            turn(d, both, True, False)
-            turn(d, neg, False, False)
+        def hpart(t3, h):
+            return planes(t3)[:, :, h * MH : (h + 1) * MH]
 
-        def mix_in(d, cols):
+        def gate_h(d, h):
             nc.vector.scalar_tensor_tensor(
-                mixes[d][:, cols], boths[d][:, cols], stat4[:, d : d + 1], mixes[d - 1][:, cols], ALU.mult, ALU.add
+                hpart(boths[d], h), hpart(gates[d], h), 2.0, dealt(hbanks[h][:, halves[d]]), ALU.add, ALU.mult
             )
 
-        stream(0)
-        nc.gpsimd.tensor_scalar(mixes[0][:], boths[0][:], stat4[:, 0:1], 0.0, ALU.mult, ALU.add)
-        stream(1)
+        def neg_h(d, h):
+            nc.scalar.activation(hpart(negs[d], h), dealt(hbanks[h][:, halves[d]]), ACT.Copy, scale=-1.0)
+
+        def stream(d):
+            nc.vector.scalar_tensor_tensor(planes(boths[d]), planes(gates[d]), 2.0, dealt(hbanks[d][:]), ALU.add, ALU.mult)
+            nc.scalar.activation(planes(negs[d]), dealt(hbanks[d][:]), ACT.Copy, scale=-1.0)
+
+        def mix_in(d, view):
+            nc.vector.scalar_tensor_tensor(
+                view(mixes[d]), view(boths[d]), stat4[:, d : d + 1], view(mixes[d - 1]), ALU.mult, ALU.add
+            )
+
+        gate_h(0, 0)
+        nc.gpsimd.tensor_scalar(hpart(mixes[0], 0), hpart(boths[0], 0), stat4[:, 0:1], 0.0, ALU.mult, ALU.add)
+        gate_h(1, 0)
+        neg_h(0, 0)
+        neg_h(1, 0)
+        mix_in(1, lambda t3: hpart(t3, 0))
+        gate_h(0, 1)
+        nc.gpsimd.tensor_scalar(hpart(mixes[0], 1), hpart(boths[0], 1), stat4[:, 0:1], 0.0, ALU.mult, ALU.add)
+        gate_h(1, 1)
+        neg_h(0, 1)
+        neg_h(1, 1)
         stream(2)
-        mix_in(1, slice(0, H))
+        mix_in(1, lambda t3: hpart(t3, 1))
         stream(3)
         for d in (2, 3):
             for cols in halves:
-                mix_in(d, cols)
+                mix_in(d, lambda t3: t3[:, cols])
+        for d in range(D):
+            turn(d, boths[d], True, False)
+            turn(d, negs[d], False, False)
 
         wo_bf = cast("wo_bf", wo_raw, N, 0)
-        wo_codes = tile("wo_codes", [P, N], U32)
+        wo_codes = tile("wo_codes", [P, N], U32, tag="mix2")
         wo_scales = tile("wo_scales", [P, N], U8)
         quantize(wo_codes[:], wo_scales[:], wo_bf)
 
@@ -190,8 +211,10 @@ def tile_picked_yhyper_back_p_kernel(
             if d == 0:
                 for cols in halves:
                     nc.vector.tensor_scalar(back[:, cols], mid[:, cols], depth4[:, 0:1], None, ALU.mult)
-            elif d == 1:
-                nc.vector.tensor_scalar(back[:], mid[:], depth4[:, 1:2], None, ALU.mult)
+            elif d == 2:
+                nc.vector.tensor_scalar(back[:], mid[:], depth4[:, 2:3], None, ALU.mult)
+            elif d == 3:
+                nc.gpsimd.tensor_scalar(back[:], mid[:], depth4[:, 3:4], 0.0, ALU.mult, ALU.add)
             else:
                 nc.scalar.activation(back[:], mid[:], ACT.Copy, scale=depth4[:, d : d + 1])
             turn(d, back, False, True)
@@ -226,15 +249,21 @@ def tile_picked_yhyper_back_p_kernel(
                     stop=True,
                 )
 
+        flat = tile("flat", [P, PACK, V], BF16)
+        for t in range(PACK):
+            nc.scalar.activation(flat[:, t, :], zbanks[1][:, t * P : (t + 1) * P], ACT.Copy, scale=unit4[:, t : t + 1])
+        nc.scalar.copy(
+            zzs[1][:].rearrange("p (c i) t -> p c t i", i=4), flat[:].rearrange("p t (c i) -> p c t i", i=4)
+        )
         scale_out(0, slice(0, V))
-        for d in range(1, D - 1):
-            scale_out(d, slice(0, V))
-            readout(d - 1, slice(0, V))
-        scale_out(D - 1, slice(0, VH))
-        readout(D - 2, slice(0, V))
-        scale_out(D - 1, slice(VH, V))
-        readout(D - 1, slice(0, VH))
-        readout(D - 1, slice(VH, V))
+        scale_out(2, slice(0, V))
+        readout(0, slice(0, V))
+        scale_out(3, slice(0, VH))
+        readout(2, slice(0, V))
+        scale_out(3, slice(VH, V))
+        readout(1, slice(0, V))
+        readout(3, slice(0, VH))
+        readout(3, slice(VH, V))
         for g in range(2):
             result = tile(f"result{g}", [P, VH, D], F32)
             src = obanks[g][:, : D * VH].rearrange("p (d v) -> p v d", d=D)

@@ -151,7 +151,7 @@ def tile_picked_yhyper_back_p_kernel(
                 )
 
         boths = [tile(f"both{d}", [P, H], F32) for d in range(D)]
-        negs = [tile(f"neg{d}", [P, H], F32) for d in range(D)]
+        negs = [tile(f"neg{d}", [P, H], F32) for d in range(D - 1)]
         mixes = [tile(f"mix{d}", [P, H], F32) for d in range(D)]
         MH = P // 2
 
@@ -188,13 +188,18 @@ def tile_picked_yhyper_back_p_kernel(
         neg_h(1, 1)
         stream(2)
         mix_in(1, lambda t3: hpart(t3, 1))
-        stream(3)
+        nc.vector.scalar_tensor_tensor(planes(boths[3]), planes(gates[3]), 2.0, dealt(hbanks[3][:]), ALU.add, ALU.mult)
         for d in (2, 3):
             for cols in halves:
                 mix_in(d, lambda t3: t3[:, cols])
+        spare = bank("spare", "b2")
+        product(spare[:], "w1", 3, whole)
+        product(spare[:], "w1", 3, whole)
+        product(spare[:, 0:64], "w1", 3, slice(0, 64))
         for d in range(D):
             turn(d, boths[d], True, False)
-            turn(d, negs[d], False, False)
+            if d < D - 1:
+                turn(d, negs[d], False, False)
 
         wo_bf = cast("wo_bf", wo_raw, N, 0)
         wo_codes = tile("wo_codes", [P, N], U32, tag="mix2")
@@ -212,9 +217,11 @@ def tile_picked_yhyper_back_p_kernel(
                 for cols in halves:
                     nc.vector.tensor_scalar(back[:, cols], mid[:, cols], depth4[:, 0:1], None, ALU.mult)
             elif d == 2:
-                nc.vector.tensor_scalar(back[:], mid[:], depth4[:, 2:3], None, ALU.mult)
+                nc.gpsimd.tensor_scalar(back[:], mid[:], depth4[:, 2:3], 0.0, ALU.mult, ALU.add)
             elif d == 3:
-                nc.gpsimd.tensor_scalar(back[:], mid[:], depth4[:, 3:4], 0.0, ALU.mult, ALU.add)
+                nc.vector.scalar_tensor_tensor(
+                    planes(back), planes(mid), depth4[:, 3:4], dealt(hbanks[3][:]), ALU.mult, ALU.subtract
+                )
             else:
                 nc.scalar.activation(back[:], mid[:], ACT.Copy, scale=depth4[:, d : d + 1])
             turn(d, back, False, True)

from contextlib import ExitStack

import concourse.mybir as mybir
from concourse.masks import make_identity

F32 = mybir.dt.float32
BF16 = mybir.dt.bfloat16
I32 = mybir.dt.int32
U32 = mybir.dt.uint32
U16 = mybir.dt.uint16
U8 = mybir.dt.uint8
FP8X4 = mybir.dt.float8_e4m3fn_x4
ACT = mybir.ActivationFunctionType
ALU = mybir.AluOpType

P = 128
PACK = 4
K, T, S, D, N, H = 512, 1024, 512, 4, 128, 512
V = S // D
HALF = H // 2
FLOPS = 2 * K * H * S * 2 + 2 * H * N * S


def tile_picked_yhyper_back_p_kernel(
    tc, x_words, x_scales, w1, wg, stat, depth, unit, wo, offs, out
):
    nc = tc.nc
    with ExitStack() as ctx:
        sb = ctx.enter_context(tc.tile_pool(name="sb", bufs=1))
        ps = ctx.enter_context(tc.psum_pool(name="ps", bufs=1))

        def tile(name, shape, dtype, tag=None):
            return sb.tile(shape, dtype, name=name, tag=tag or name, align_bytes=64)

        def bank(name, tag):
            return ps.tile([P, 512], F32, name=name, tag=tag)

        offsets = sb.tile([P, S // 16], U16, name="offsets")
        xw = tile("xw", [P, T], U32)
        xs = tile("xs", [P, T], U8)
        nc.gpsimd.memset(xs[:].bitcast(I32), 0)
        zero = tile("zero", [P, 1], F32)
        nc.gpsimd.memset(zero[:], 0.0)
        nc.sync.dma_start(out=xw[:].bitcast(I32), in_=x_words[0].rearrange("p n t -> p (n t)").bitcast(I32))
        nc.sync.dma_start(offsets[:], offs)
        for q in range(4):
            nc.sync.dma_start(
                out=xs[32 * q : 32 * q + 4, :].bitcast(I32), in_=x_scales[0, 4 * q : 4 * q + 4, :].bitcast(I32)
            )
        raws = {}
        for name, w in (("wg", wg), ("w1", w1)):
            for h in range(2):
                raw = tile(f"{name}_raw{h}", [P, PACK, HALF], F32)
                nc.sync.dma_start(out=raw[:], in_=w[:, h * HALF : (h + 1) * HALF].rearrange("(p j) c -> p j c", j=PACK))
                raws[name, h] = raw
        stat4 = tile("stat4", [P, D], F32)
        nc.sync.dma_start(out=stat4[:], in_=stat[0, :].rearrange("(v d) -> v d", d=D))
        wo_raw = tile("wo_raw", [P, PACK, N], F32)
        nc.sync.dma_start(out=wo_raw[:], in_=wo.rearrange("(p j) c -> p j c", j=PACK))
        depth4 = tile("depth4", [P, D], F32)
        nc.sync.dma_start(out=depth4[:], in_=depth[0, :].rearrange("(v d) -> v d", d=D))
        unit4 = tile("unit4", [P, PACK], F32)
        nc.sync.dma_start(out=unit4[:], in_=unit.rearrange("(p t) o -> p (t o)", t=PACK))

        ident = tile("ident", [P, P], F32)
        make_identity(nc, ident[:])
        warm = tile("warm", [P, 1], F32)
        nc.scalar.activation(warm[:], zero[:], ACT.Silu)

        xg = tile("xg", [P, S], U32)
        nc.vector.tensor_copy(xg[:].rearrange("p (d v) -> p v d", d=D), xw[:].indirect(offsets[:]))
        sg = tile("sg", [P, S], U8)
        nc.vector.tensor_copy(sg[:], xs[:].indirect(offsets[:]))
        sd = tile("sd", [P, S], U8)
        nc.vector.tensor_copy(sd[:].rearrange("p (d v) -> p d v", d=D), sg[:].rearrange("p (v d) -> p d v", d=D))

        def cast(name, raw, width, on_vector):
            grouped = tile(name, [P, width, PACK], BF16)
            dst = grouped[:].rearrange("p (c i) t -> p c t i", i=4)
            src = raw[:].rearrange("p t (c i) -> p c t i", i=4)
            cut = on_vector // 4
            if cut > 0:
                nc.vector.tensor_copy(dst[:, :cut], src[:, :cut])
            if on_vector < width:
                nc.scalar.copy(dst[:, cut:], src[:, cut:])
            return grouped

        def quantize(codes, scales, grouped):
            nc.vector.quantize_mx(out=codes.bitcast(FP8X4), scales=scales, in_=grouped[:].rearrange("p c t -> p (c t)"))

        on_vector = {("wg", 0): 0, ("wg", 1): 0, ("w1", 0): 128, ("w1", 1): 160}
        wq = {}
        for name in ("wg", "w1"):
            codes = tile(f"{name}_codes", [P, H], U32)
            scales = tile(f"{name}_scales", [P, H], U8)
            for h in range(2):
                grouped = cast(f"{name}_bf{h}", raws[name, h], HALF, on_vector[name, h])
                cols = slice(h * HALF, (h + 1) * HALF)
                quantize(codes[:, cols], scales[:, cols], grouped)
            wq[name] = (codes, scales)

        halves = [slice(0, HALF), slice(HALF, H)]
        whole = slice(0, H)

        def product(dst, name, d, part):
            cols = slice(d * V, (d + 1) * V)
            nc.tensor.matmul_mx(
                out=dst,
                lhsT=xg[:, cols].bitcast(FP8X4),
                lhsT_scale=sd[:, cols],
                rhs=wq[name][0][:, part].bitcast(FP8X4),
                rhs_scale=wq[name][1][:, part],
                start=True,
                stop=True,
            )

        def dealt(acc):
            return acc.rearrange("p (m t) -> p t m", t=PACK)

        def planes(t3):
            return t3[:].rearrange("p (t m) -> p t m", t=PACK)

        gbanks = [bank(f"g{d}", f"a{d}") for d in range(2)]
        hbanks = [bank(f"h{d}", f"b{d}") for d in range(D)]
        gates = [tile(f"gate{d}", [P, H], F32) for d in range(D)]
        for part in halves:
            for d in (0, 1):
                product(gbanks[d][:, part], "wg", d, part)
        for h in range(2):
            for d in (0, 1):
                product(hbanks[h][:, halves[d]], "w1", d, halves[h])
        for d in (0, 1):
            nc.scalar.activation(planes(gates[d]), dealt(gbanks[d][:]), ACT.Tanh)
        for d in (2, 3):
            gbanks.append(bank(f"g{d}", f"a{d - 2}"))
            product(gbanks[d][:], "wg", d, whole)
            product(hbanks[d][:], "w1", d, whole)
            nc.scalar.activation(planes(gates[d]), dealt(gbanks[d][:]), ACT.Tanh)

        zbanks = [bank(f"z{d}", f"a{(d + 2) % D}") for d in range(D)]

        def turn(d, src, first, last):
            for t in range(PACK):
                nc.tensor.matmul(
                    zbanks[d][:, t * P : (t + 1) * P],
                    src[:, t * P : (t + 1) * P],
                    ident[:],
                    start=(first and t == 0),
                    stop=(last and t == PACK - 1),
                    is_transpose=True,
                )

        boths = [tile(f"both{d}", [P, H], F32) for d in range(D)]
        negs = [tile(f"neg{d}", [P, H], F32) for d in range(D - 1)]
        mixes = [tile(f"mix{d}", [P, H], F32) for d in range(D)]
        MH = P // 2

        def hpart(t3, h):
            return planes(t3)[:, :, h * MH : (h + 1) * MH]

        def gate_h(d, h):
            nc.vector.scalar_tensor_tensor(
                hpart(boths[d], h), hpart(gates[d], h), 2.0, dealt(hbanks[h][:, halves[d]]), ALU.add, ALU.mult
            )

        def neg_h(d, h):
            nc.scalar.activation(hpart(negs[d], h), dealt(hbanks[h][:, halves[d]]), ACT.Copy, scale=-1.0)

        def stream(d):
            nc.vector.scalar_tensor_tensor(planes(boths[d]), planes(gates[d]), 2.0, dealt(hbanks[d][:]), ALU.add, ALU.mult)
            nc.scalar.activation(planes(negs[d]), dealt(hbanks[d][:]), ACT.Copy, scale=-1.0)

        def mix_in(d, view):
            nc.vector.scalar_tensor_tensor(
                view(mixes[d]), view(boths[d]), stat4[:, d : d + 1], view(mixes[d - 1]), ALU.mult, ALU.add
            )

        gate_h(0, 0)
        nc.gpsimd.tensor_scalar(hpart(mixes[0], 0), hpart(boths[0], 0), stat4[:, 0:1], 0.0, ALU.mult, ALU.add)
        gate_h(1, 0)
        neg_h(0, 0)
        neg_h(1, 0)
        mix_in(1, lambda t3: hpart(t3, 0))
        gate_h(0, 1)
        nc.gpsimd.tensor_scalar(hpart(mixes[0], 1), hpart(boths[0], 1), stat4[:, 0:1], 0.0, ALU.mult, ALU.add)
        gate_h(1, 1)
        neg_h(0, 1)
        neg_h(1, 1)
        stream(2)
        mix_in(1, lambda t3: hpart(t3, 1))
        nc.vector.scalar_tensor_tensor(planes(boths[3]), planes(gates[3]), 2.0, dealt(hbanks[3][:]), ALU.add, ALU.mult)
        for d in (2, 3):
            for cols in halves:
                mix_in(d, lambda t3: t3[:, cols])
        spare = bank("spare", "b2")
        product(spare[:], "w1", 3, whole)
        product(spare[:], "w1", 3, whole)
        product(spare[:, 0:64], "w1", 3, slice(0, 64))
        for d in range(D):
            turn(d, boths[d], True, False)
            if d < D - 1:
                turn(d, negs[d], False, False)

        wo_bf = cast("wo_bf", wo_raw, N, 0)
        wo_codes = tile("wo_codes", [P, N], U32, tag="mix2")
        wo_scales = tile("wo_scales", [P, N], U8)
        quantize(wo_codes[:], wo_scales[:], wo_bf)

        mid = tile("mid", [P, H], F32)
        for cols in halves:
            nc.scalar.activation(mid[:, cols], mixes[3][:, cols], ACT.Silu, scale=0.5)

        obanks = [bank("o0", "b0"), bank("o1", "b1")]
        for d in range(D):
            back = tile(f"back{d}", [P, H], F32)
            if d == 0:
                for cols in halves:
                    nc.vector.tensor_scalar(back[:, cols], mid[:, cols], depth4[:, 0:1], None, ALU.mult)
            elif d == 2:
                nc.gpsimd.tensor_scalar(back[:], mid[:], depth4[:, 2:3], 0.0, ALU.mult, ALU.add)
            elif d == 3:
                nc.vector.scalar_tensor_tensor(
                    planes(back), planes(mid), depth4[:, 3:4], dealt(hbanks[3][:]), ALU.mult, ALU.subtract
                )
            else:
                nc.scalar.activation(back[:], mid[:], ACT.Copy, scale=depth4[:, d : d + 1])
            turn(d, back, False, True)
        VH = V // 2
        zzs = [tile(f"zz{d}", [P, V, PACK], BF16) for d in range(D)]
        z_codes = [tile(f"z_codes{d}", [P, V], U32) for d in range(D)]
        z_scales = [tile(f"z_scales{d}", [P, V], U8) for d in range(D)]

        def scale_out(d, vs):
            n = vs.stop - vs.start
            nc.vector.tensor_tensor(
                zzs[d][:, vs, :],
                zbanks[d][:].rearrange("p (t v) -> p v t", t=PACK)[:, vs, :],
                unit4[:].unsqueeze(1).to_broadcast([P, n, PACK]),
                ALU.mult,
            )

        def readout(d, vs):
            nc.vector.quantize_mx(
                out=z_codes[d][:, vs].bitcast(FP8X4),
                scales=z_scales[d][:, vs],
                in_=zzs[d][:, vs, :].rearrange("p c t -> p (c t)"),
            )
            for g in range(vs.start // VH, vs.stop // VH):
                nc.tensor.matmul_mx(
                    out=obanks[g][:, d * VH : (d + 1) * VH],
                    lhsT=wo_codes[:].bitcast(FP8X4),
                    lhsT_scale=wo_scales[:],
                    rhs=z_codes[d][:, g * VH : (g + 1) * VH].bitcast(FP8X4),
                    rhs_scale=z_scales[d][:, g * VH : (g + 1) * VH],
                    start=True,
                    stop=True,
                )

        flat = tile("flat", [P, PACK, V], BF16)
        for t in range(PACK):
            nc.scalar.activation(flat[:, t, :], zbanks[1][:, t * P : (t + 1) * P], ACT.Copy, scale=unit4[:, t : t + 1])
        nc.scalar.copy(
            zzs[1][:].rearrange("p (c i) t -> p c t i", i=4), flat[:].rearrange("p t (c i) -> p c t i", i=4)
        )
        scale_out(0, slice(0, V))
        scale_out(2, slice(0, V))
        readout(0, slice(0, V))
        scale_out(3, slice(0, VH))
        readout(2, slice(0, V))
        scale_out(3, slice(VH, V))
        readout(1, slice(0, V))
        readout(3, slice(0, VH))
        readout(3, slice(VH, V))
        for g in range(2):
            result = tile(f"result{g}", [P, VH, D], F32)
            src = obanks[g][:, : D * VH].rearrange("p (d v) -> p v d", d=D)
            if g == 0:
                nc.scalar.copy(result[:], src)
                queue = nc.scalar
            else:
                nc.vector.tensor_copy(result[:], src)
                queue = nc.sync
            queue.dma_start(out=out[:, g * HALF : (g + 1) * HALF], in_=result[:].rearrange("p v d -> p (v d)"))
